import numpy as np
import ml_dtypes


def mxq(x, axis, fmt="e4m3"):
    dtype, down = {"e4m3": (ml_dtypes.float8_e4m3fn, 7), "e5m2": (ml_dtypes.float8_e5m2, 14)}[fmt]
    v = np.moveaxis(np.asarray(x, np.float32).astype(ml_dtypes.bfloat16).astype(np.float64), axis, -1)
    blocks = v.reshape(v.shape[:-1] + (-1, 32))
    amax = np.abs(blocks).max(-1, keepdims=True)
    byte = np.maximum(np.where(amax > 0, np.frexp(amax)[1] - 1 + 127, 0) - down, 1)
    scale = np.exp2(byte - 127.0)
    codes = (blocks / scale).astype(np.float32).astype(dtype).astype(np.float64)
    return np.moveaxis((codes * scale).reshape(v.shape), -1, axis)


WIDE = False


def mx_kscale(k):
    if not WIDE:
        return np.ones(k)
    levels = np.array([10, -10, 5, -5, 0])
    if k % 512:
        return np.exp2(np.random.permutation(np.resize(levels, k // 32))).repeat(32)
    a = np.empty((k // 512, 16))
    for p in range(k // 512):
        a[p, :8] = np.random.permutation(np.resize(levels, 8))
        for g in range(8):
            far = levels[np.abs(levels - a[p, g]) >= 10]
            a[p, g + 8] = far[np.random.randint(len(far))]
    return np.exp2(a.ravel()).repeat(32)


def f64(x):
    return np.asarray(x).astype(np.float64)


def striped(idx):
    return np.tile(np.asarray(idx).reshape(-1, 16).T, (8, 1)).astype(np.uint16)


def unstriped(offs):
    return offs[:16].T.reshape(-1).astype(np.int64)


E2M1 = np.array([0.0, 0.5, 1.0, 1.5, 2.0, 3.0, 4.0, 6.0, -0.0, -0.5, -1.0, -1.5, -2.0, -3.0, -4.0, -6.0])


def pack_weight(w, fmt):
    k, n = w.shape
    w = f64(np.asarray(w, np.float32).astype(ml_dtypes.bfloat16)).reshape(k // 32, 32, n)
    amax = np.abs(w).max(1)
    if fmt == "e4m3":
        byte = np.frexp(amax)[1] - 1 + 127 - 7
    else:
        mant, ex = np.frexp(amax / 6.0)
        byte = np.where(mant > 0.5, ex, ex - 1) + 127
    byte = np.clip(np.where(amax > 0, byte, 1), 1, 254)
    scaled = (w * np.exp2(127.0 - byte)[:, None, :]).reshape(k, n).astype(np.float32)
    by_word = np.ascontiguousarray(scaled.reshape(k // 512, 128, 4, n).transpose(0, 1, 3, 2))
    if fmt == "e4m3":
        words = by_word.astype(ml_dtypes.float8_e4m3fn).view(np.uint8)
    else:
        c = by_word.astype(ml_dtypes.float4_e2m1fn).view(np.uint8) & 0xF
        words = (c[..., 0::2] | (c[..., 1::2] << 4)).reshape(k // 512, 128, 2 * n)
    return np.ascontiguousarray(words), np.ascontiguousarray(byte.astype(np.uint8).reshape(k // 512, 16, n))


def unpack_weight(words, scales, fmt):
    g, _, n = scales.shape
    words = np.ascontiguousarray(words).reshape(g, 128, n, -1)
    if fmt == "e4m3":
        vals = words.view(ml_dtypes.float8_e4m3fn).astype(np.float64)
    else:
        nib = np.empty((g, 128, n, 4), np.uint8)
        nib[..., 0::2] = words & 0xF
        nib[..., 1::2] = words >> 4
        vals = E2M1[nib]
    vals = vals * np.repeat(np.exp2(scales.astype(np.float64) - 127.0), 8, axis=1)[..., None]
    return vals.transpose(0, 1, 3, 2).reshape(g * 512, n)


D, T, I, Q, G, M = 512, 2048, 512, 128, 64, 512


def setup_inputs():
    n = np.random.standard_normal
    idx = np.random.permutation(T)[:I]
    idx2 = np.random.permutation(T)[:I]
    idx3 = np.random.permutation(M)[:G]
    fd = mx_kscale(D)
    keysp = pack_weight(n((D, T)) / fd[:, None], "e2m1")
    return {
        "query": (n((D, Q)) * 1.0 / np.sqrt(D) * fd[:, None]).astype(np.float32),
        "query2": (n((D, Q)) * 1.0 / np.sqrt(D) * fd[:, None]).astype(np.float32),
        "keys_words": keysp[0],
        "keys_scales": keysp[1],
        "lam": (np.random.uniform(1.0, 3.0, (Q, 1))).astype(np.float32),
        "width": (np.random.uniform(0.3, 0.8, (Q, 1))).astype(np.float32),
        "worth": np.tile(np.random.uniform(0.2, 2.0, T), (128, 1)).astype(np.float32),
        "old": (1.0 * n((Q, M))).astype(np.float32),
        "offs": striped(idx),
        "offs2": striped(idx2),
        "offs3": striped(idx3),
    }


def reference(query, query2, keys_words, keys_scales, lam, width, worth, old, offs, offs2, offs3):
    idx = unstriped(offs)
    idx2 = unstriped(offs2)
    idx3 = unstriped(offs3)
    keysu = unpack_weight(keys_words, keys_scales, "e2m1")
    queryq = mxq(f64(query), 0, "e4m3")
    a = queryq.T @ keysu
    query2q = mxq(f64(query2), 0, "e4m3")
    b = query2q.T @ keysu
    la = np.square(a[:, idx]) + np.square(b[:, idx])
    lb = np.square(a[:, idx2]) + np.square(b[:, idx2])
    s = (a[:, idx] * a[:, idx2] + b[:, idx] * b[:, idx2]) / np.sqrt(la * lb + 0.5) * f64(lam)
    ce = (s - np.mean(s, axis=1, keepdims=True)) / f64(width)
    p = 1.0 / (np.square(ce) + 1.0)
    w = p / np.sum(p, axis=1, keepdims=True)
    ws = w * f64(worth)[:1][:, idx] * 512.0
    wp = ws.reshape(Q, G, I // G).sum(axis=2)
    wf = np.zeros((Q, M))
    wf[:, idx3] = wp
    y = f64(old) + wf
    return y

@@ -1,0 +1,165 @@
+from contextlib import ExitStack
+
+import concourse.mybir as mybir
+
+F32 = mybir.dt.float32
+BF16 = mybir.dt.bfloat16
+U32 = mybir.dt.uint32
+I32 = mybir.dt.int32
+U16 = mybir.dt.uint16
+U8 = mybir.dt.uint8
+FP8X4 = mybir.dt.float8_e4m3fn_x4
+FP4X4 = mybir.dt.float4_e2m1fn_x4
+ACT = mybir.ActivationFunctionType
+ALU = mybir.AluOpType
+AX = mybir.AxisListType
+
+P = 128
+PACK = 4
+D, T, SLOTS, Q, RUNS, COLS = 512, 2048, 512, 128, 64, 512
+RUN = SLOTS // RUNS
+N = 512
+BANKS = T // N
+FLOPS = 2 * 2 * D * Q * T
+
+
+def tile_attend_planecos_typical_pagesums_kernel(
+    tc, query, query2, keys_words, keys_scales, lam, width, worth, old, offs, offs2, offs3, out
+):
+    nc = tc.nc
+    with ExitStack() as ctx:
+        sb = ctx.enter_context(tc.tile_pool(name="sb", bufs=1))
+        psum = ctx.enter_context(tc.psum_pool(name="psum", bufs=1))
+
+        key_scales = sb.tile([P, T], U8, align_bytes=64)
+        nc.vector.memset(key_scales[:].bitcast(I32), 0)
+        warm = sb.tile([P, 1], F32)
+        warm_out = sb.tile([P, 1], F32)
+        nc.vector.memset(warm[:], 1.0)
+
+        raw = [sb.tile([P, PACK, Q], F32, name=f"raw{i}") for i in range(2)]
+        keys = [sb.tile([P, T], U8, align_bytes=64, name=f"keys{h}") for h in range(2)]
+        nc.sync.dma_start(out=raw[0][:], in_=query.rearrange("(p j) w -> p j w", j=PACK))
+        for quad in range(4):
+            (nc.scalar if quad < 2 else nc.sync).dma_start(
+                out=key_scales[32 * quad : 32 * quad + 4, :].bitcast(I32),
+                in_=keys_scales[0, 4 * quad : 4 * quad + 4, :].bitcast(I32),
+            )
+        nc.scalar.activation(warm_out[:], warm[:], ACT.Abs_reciprocal_sqrt)
+        for h, queue in enumerate((nc.sync, nc.gpsimd)):
+            queue.dma_start(out=keys[h][:].bitcast(I32), in_=keys_words[0][:, h * T : (h + 1) * T].bitcast(I32))
+        nc.gpsimd.dma_start(out=raw[1][:], in_=query2.rearrange("(p j) w -> p j w", j=PACK))
+
+        list1 = sb.tile([P, SLOTS // 16], U16)
+        list2 = sb.tile([P, SLOTS // 16], U16)
+        list3 = sb.tile([P, RUNS // 16], U16)
+        nc.sync.dma_start(list1[:], offs)
+        nc.sync.dma_start(list2[:], offs2)
+        nc.sync.dma_start(list3[:], offs3)
+
+        placed = sb.tile([P, COLS], F32)
+        nc.vector.memset(placed[:], 0.0)
+
+        codes, scales = [], []
+        for i in range(2):
+            grouped = sb.tile([P, Q, PACK], BF16, align_bytes=64, name=f"grouped{i}")
+            nc.vector.tensor_copy(out=grouped[:], in_=raw[i][:].rearrange("p j w -> p w j"))
+            codes.append(sb.tile([P, Q], U32, align_bytes=64, name=f"codes{i}"))
+            scales.append(sb.tile([P, Q], U8, align_bytes=64, name=f"scales{i}"))
+            nc.vector.quantize_mx(
+                out=codes[i][:].bitcast(FP8X4), scales=scales[i][:], in_=grouped[:].rearrange("p w j -> p (w j)")
+            )
+
+        worth_sb = sb.tile([P, T], F32, name="raw0")
+        nc.sync.dma_start(worth_sb[:], worth)
+        lam_sb = sb.tile([P, 1], F32, name="warm")
+        width_sb = sb.tile([P, 1], F32, name="warm_out")
+        nc.sync.dma_start(lam_sb[:], lam)
+        nc.sync.dma_start(width_sb[:], width)
+        old_sb = sb.tile([P, COLS], F32, name="raw1")
+        nc.sync.dma_start(old_sb[:], old)
+
+        width2 = sb.tile([P, 1], F32)
+        nc.gpsimd.tensor_tensor(width2[:], width_sb[:], width_sb[:], ALU.mult)
+
+        coords = [sb.tile([P, T], F32, name=f"coord{i}") for i in range(2)]
+        for i in range(2):
+            for c in range(BANKS):
+                bank = psum.tile([P, N], F32, name=f"bank{i}_{c}")
+                nc.tensor.matmul_mx(
+                    out=bank[:],
+                    lhsT=codes[i][:].bitcast(FP8X4),
+                    lhsT_scale=scales[i][:],
+                    rhs=keys[c // 2][:, (c % 2) * 2 * N : (c % 2 + 1) * 2 * N].bitcast(FP4X4),
+                    rhs_scale=key_scales[:, c * N : (c + 1) * N],
+                    start=True,
+                    stop=True,
+                )
+                dst = coords[i][:, c * N : (c + 1) * N]
+                if i == 0 and c % 2 == 1:
+                    nc.vector.tensor_copy(out=dst, in_=bank[:])
+                else:
+                    nc.scalar.copy(out=dst, in_=bank[:])
+
+        def slot_tile(name):
+            return sb.tile([P, SLOTS], F32, name=name)
+
+        a1, a2, b1, b2 = (slot_tile(n) for n in ("a1", "a2", "b1", "b2"))
+        sq = {n: slot_tile("sq_" + n) for n in ("a1", "a2", "b1", "b2")}
+        for name, tile, window, offsets in (
+            ("a1", a1, coords[0], list1),
+            ("a2", a2, coords[0], list2),
+            ("b1", b1, coords[1], list1),
+            ("b2", b2, coords[1], list2),
+        ):
+            nc.vector.tensor_copy(tile[:], window[:].indirect(offsets[:]))
+            nc.scalar.activation(sq[name][:], tile[:], ACT.Square)
+
+
+        aa, bb, dot, len1, len2, lens, inv_len, score = (
+            slot_tile(n) for n in ("aa", "bb", "dot", "len1", "len2", "lens", "inv_len", "score")
+        )
+        halves = [slice(0, SLOTS // 2), slice(SLOTS // 2, SLOTS)]
+        nc.vector.tensor_tensor(aa[:], a1[:], a2[:], ALU.mult)
+        nc.vector.tensor_tensor(len1[:], sq["a1"][:], sq["b1"][:], ALU.add)
+        nc.vector.tensor_tensor(len2[:], sq["a2"][:], sq["b2"][:], ALU.add)
+        nc.vector.tensor_tensor(bb[:], b1[:], b2[:], ALU.mult)
+        for h in halves:
+            nc.vector.tensor_tensor(lens[:, h], len1[:, h], len2[:, h], ALU.mult)
+            nc.scalar.activation(inv_len[:, h], lens[:, h], ACT.Abs_reciprocal_sqrt, bias=0.5)
+        nc.vector.tensor_tensor(dot[:], aa[:], bb[:], ALU.add)
+        score_sum = sb.tile([P, 1], F32)
+        nc.vector.scalar_tensor_tensor(
+            score[:], dot[:], lam_sb[:], inv_len[:], ALU.mult, ALU.mult, accum_out=score_sum[:]
+        )
+
+        slot_worth = slot_tile("dot")
+        nc.vector.tensor_copy(slot_worth[:], worth_sb[:].indirect(list1[:]))
+
+        dev2, root, part, weighed = (slot_tile(n) for n in ("dev2", "root", "part", "weighed"))
+        part_sums = [sb.tile([P, 1], F32, name=f"part_sum{i}") for i in range(2)]
+        run_sums = sb.tile([P, RUNS], F32)
+        for h in halves:
+            nc.scalar.activation(dev2[:, h], score[:, h], ACT.Square, bias=score_sum[:], scale=-float(SLOTS))
+        for h in halves:
+            nc.scalar.activation(root[:, h], dev2[:, h], ACT.Abs_reciprocal_sqrt, bias=width2[:], scale=1.0 / (SLOTS * SLOTS))
+        for i, h in enumerate(halves):
+            nc.scalar.activation(part[:, h], root[:, h], ACT.Square, accum_out=part_sums[i][:])
+        for h in halves:
+            nc.vector.tensor_tensor(weighed[:, h], part[:, h], slot_worth[:, h], ALU.mult)
+        for i, h in enumerate(halves):
+            nc.vector.tensor_reduce(
+                run_sums[:, i * RUNS // 2 : (i + 1) * RUNS // 2],
+                weighed[:, h].rearrange("p (g r) -> p g r", r=RUN),
+                AX.X,
+                ALU.add,
+            )
+        mean_part = sb.tile([P, 1], F32)
+        nc.vector.tensor_scalar(mean_part[:], part_sums[0][:], part_sums[1][:], 1.0 / SLOTS, ALU.add, ALU.mult)
+        norm = sb.tile([P, 1], F32)
+        nc.vector.reciprocal(norm[:], mean_part[:])
+        nc.vector.tensor_copy(placed[:].indirect(list3[:]), run_sums[:])
+        result = sb.tile([P, COLS], F32)
+        for h, queue in zip(halves, (nc.sync, nc.scalar)):
+            nc.vector.scalar_tensor_tensor(result[:, h], placed[:, h], norm[:], old_sb[:, h], ALU.mult, ALU.add)
+            queue.dma_start(out[:, h], result[:, h])

@@ -32,7 +32,6 @@ def tile_attend_planecos_typical_pagesums_kernel(
         psum = ctx.enter_context(tc.psum_pool(name="psum", bufs=1))
 
         key_scales = sb.tile([P, T], U8, align_bytes=64)
-        nc.vector.memset(key_scales[:].bitcast(I32), 0)
         warm = sb.tile([P, 1], F32)
         warm_out = sb.tile([P, 1], F32)
         nc.vector.memset(warm[:], 1.0)
@@ -41,14 +40,14 @@ def tile_attend_planecos_typical_pagesums_kernel(
         keys = [sb.tile([P, T], U8, align_bytes=64, name=f"keys{h}") for h in range(2)]
         nc.sync.dma_start(out=raw[0][:], in_=query.rearrange("(p j) w -> p j w", j=PACK))
         for quad in range(4):
-            (nc.scalar if quad < 2 else nc.sync).dma_start(
+            nc.sync.dma_start(
                 out=key_scales[32 * quad : 32 * quad + 4, :].bitcast(I32),
                 in_=keys_scales[0, 4 * quad : 4 * quad + 4, :].bitcast(I32),
             )
         nc.scalar.activation(warm_out[:], warm[:], ACT.Abs_reciprocal_sqrt)
-        for h, queue in enumerate((nc.sync, nc.gpsimd)):
+        for h, queue in enumerate((nc.sync, nc.sync)):
             queue.dma_start(out=keys[h][:].bitcast(I32), in_=keys_words[0][:, h * T : (h + 1) * T].bitcast(I32))
-        nc.gpsimd.dma_start(out=raw[1][:], in_=query2.rearrange("(p j) w -> p j w", j=PACK))
+        nc.sync.dma_start(out=raw[1][:], in_=query2.rearrange("(p j) w -> p j w", j=PACK))
 
         list1 = sb.tile([P, SLOTS // 16], U16)
         list2 = sb.tile([P, SLOTS // 16], U16)
@@ -70,15 +69,10 @@ def tile_attend_planecos_typical_pagesums_kernel(
                 out=codes[i][:].bitcast(FP8X4), scales=scales[i][:], in_=grouped[:].rearrange("p w j -> p (w j)")
             )
 
-        worth_sb = sb.tile([P, T], F32, name="raw0")
-        nc.sync.dma_start(worth_sb[:], worth)
         lam_sb = sb.tile([P, 1], F32, name="warm")
         width_sb = sb.tile([P, 1], F32, name="warm_out")
         nc.sync.dma_start(lam_sb[:], lam)
         nc.sync.dma_start(width_sb[:], width)
-        old_sb = sb.tile([P, COLS], F32, name="raw1")
-        nc.sync.dma_start(old_sb[:], old)
-
         width2 = sb.tile([P, 1], F32)
         nc.gpsimd.tensor_tensor(width2[:], width_sb[:], width_sb[:], ALU.mult)
 
@@ -96,44 +90,56 @@ def tile_attend_planecos_typical_pagesums_kernel(
                     stop=True,
                 )
                 dst = coords[i][:, c * N : (c + 1) * N]
-                if i == 0 and c % 2 == 1:
+                if i == 0 and c == BANKS - 1:
                     nc.vector.tensor_copy(out=dst, in_=bank[:])
                 else:
                     nc.scalar.copy(out=dst, in_=bank[:])
+
+        worth_sb = sb.tile([P, T], F32, align_bytes=64, name="codes0")
+        nc.sync.dma_start(worth_sb[:], worth)
+        old_sb = sb.tile([P, COLS], F32, align_bytes=64, name="codes1")
+        nc.sync.dma_start(old_sb[:], old)
 
         def slot_tile(name):
             return sb.tile([P, SLOTS], F32, name=name)
 
         a1, a2, b1, b2 = (slot_tile(n) for n in ("a1", "a2", "b1", "b2"))
-        sq = {n: slot_tile("sq_" + n) for n in ("a1", "a2", "b1", "b2")}
+        sq = {
+            "a1": sb.tile([P, SLOTS], F32, align_bytes=64, name="keys1"),
+            "a2": sb.tile([P, SLOTS], F32, align_bytes=64, name="key_scales"),
+            "b1": slot_tile("sq_b1"),
+            "b2": slot_tile("sq_b2"),
+        }
+        halves = [slice(0, SLOTS // 2), slice(SLOTS // 2, SLOTS)]
+        list_halves = [slice(0, SLOTS // 32), slice(SLOTS // 32, SLOTS // 16)]
         for name, tile, window, offsets in (
             ("a1", a1, coords[0], list1),
             ("a2", a2, coords[0], list2),
             ("b1", b1, coords[1], list1),
-            ("b2", b2, coords[1], list2),
         ):
             nc.vector.tensor_copy(tile[:], window[:].indirect(offsets[:]))
             nc.scalar.activation(sq[name][:], tile[:], ACT.Square)
+        for h, entries in zip(halves, list_halves):
+            nc.vector.tensor_copy(b2[:, h], coords[1][:].indirect(list2[:, entries]))
+            nc.scalar.activation(sq["b2"][:, h], b2[:, h], ACT.Square)
 
-
-        aa, bb, dot, len1, len2, lens, inv_len, score = (
-            slot_tile(n) for n in ("aa", "bb", "dot", "len1", "len2", "lens", "inv_len", "score")
+        aa, dot, len1, len2, lens, inv_len, score = (
+            slot_tile(n) for n in ("aa", "dot", "len1", "len2", "lens", "inv_len", "score")
         )
-        halves = [slice(0, SLOTS // 2), slice(SLOTS // 2, SLOTS)]
         nc.vector.tensor_tensor(aa[:], a1[:], a2[:], ALU.mult)
         nc.vector.tensor_tensor(len1[:], sq["a1"][:], sq["b1"][:], ALU.add)
-        nc.vector.tensor_tensor(len2[:], sq["a2"][:], sq["b2"][:], ALU.add)
-        nc.vector.tensor_tensor(bb[:], b1[:], b2[:], ALU.mult)
         for h in halves:
+            nc.vector.tensor_tensor(len2[:, h], sq["a2"][:, h], sq["b2"][:, h], ALU.add)
+            nc.vector.tensor_tensor(b2[:, h], b1[:, h], b2[:, h], ALU.mult)
             nc.vector.tensor_tensor(lens[:, h], len1[:, h], len2[:, h], ALU.mult)
             nc.scalar.activation(inv_len[:, h], lens[:, h], ACT.Abs_reciprocal_sqrt, bias=0.5)
-        nc.vector.tensor_tensor(dot[:], aa[:], bb[:], ALU.add)
+        nc.vector.tensor_tensor(dot[:], aa[:], b2[:], ALU.add)
         score_sum = sb.tile([P, 1], F32)
         nc.vector.scalar_tensor_tensor(
             score[:], dot[:], lam_sb[:], inv_len[:], ALU.mult, ALU.mult, accum_out=score_sum[:]
         )
 
-        slot_worth = slot_tile("dot")
+        slot_worth = slot_tile("inv_len")
         nc.vector.tensor_copy(slot_worth[:], worth_sb[:].indirect(list1[:]))
 
         dev2, root, part, weighed = (slot_tile(n) for n in ("dev2", "root", "part", "weighed"))

@@ -45,16 +45,22 @@ def tile_attend_planecos_typical_pagesums_kernel(
                 in_=keys_scales[0, 4 * quad : 4 * quad + 4, :].bitcast(I32),
             )
         nc.scalar.activation(warm_out[:], warm[:], ACT.Abs_reciprocal_sqrt)
-        for h, queue in enumerate((nc.sync, nc.sync)):
-            queue.dma_start(out=keys[h][:].bitcast(I32), in_=keys_words[0][:, h * T : (h + 1) * T].bitcast(I32))
+        key_words = keys_words[0].bitcast(I32)
+        nc.sync.dma_start(out=keys[0][:].bitcast(I32), in_=key_words[:, : T // 4])
         nc.sync.dma_start(out=raw[1][:], in_=query2.rearrange("(p j) w -> p j w", j=PACK))
+        nc.sync.dma_start(out=keys[1][:].bitcast(I32), in_=key_words[:, T // 4 :])
 
         list1 = sb.tile([P, SLOTS // 16], U16)
         list2 = sb.tile([P, SLOTS // 16], U16)
         list3 = sb.tile([P, RUNS // 16], U16)
         nc.sync.dma_start(list1[:], offs)
         nc.sync.dma_start(list2[:], offs2)
-        nc.sync.dma_start(list3[:], offs3)
+        lam_sb = sb.tile([P, 1], F32)
+        width_sb = sb.tile([P, 1], F32)
+        worth_sb = sb.tile([P, T], F32)
+        old_sb = sb.tile([P, COLS], F32)
+        for tile, source in ((list3, offs3), (width_sb, width), (lam_sb, lam), (worth_sb, worth), (old_sb, old)):
+            nc.sync.dma_start(tile[:], source)
 
         placed = sb.tile([P, COLS], F32)
         nc.vector.memset(placed[:], 0.0)
@@ -69,36 +75,31 @@ def tile_attend_planecos_typical_pagesums_kernel(
                 out=codes[i][:].bitcast(FP8X4), scales=scales[i][:], in_=grouped[:].rearrange("p w j -> p (w j)")
             )
 
-        lam_sb = sb.tile([P, 1], F32, name="warm")
-        width_sb = sb.tile([P, 1], F32, name="warm_out")
-        nc.sync.dma_start(lam_sb[:], lam)
-        nc.sync.dma_start(width_sb[:], width)
         width2 = sb.tile([P, 1], F32)
         nc.gpsimd.tensor_tensor(width2[:], width_sb[:], width_sb[:], ALU.mult)
 
         coords = [sb.tile([P, T], F32, name=f"coord{i}") for i in range(2)]
-        for i in range(2):
-            for c in range(BANKS):
-                bank = psum.tile([P, N], F32, name=f"bank{i}_{c}")
-                nc.tensor.matmul_mx(
-                    out=bank[:],
-                    lhsT=codes[i][:].bitcast(FP8X4),
-                    lhsT_scale=scales[i][:],
-                    rhs=keys[c // 2][:, (c % 2) * 2 * N : (c % 2 + 1) * 2 * N].bitcast(FP4X4),
-                    rhs_scale=key_scales[:, c * N : (c + 1) * N],
-                    start=True,
-                    stop=True,
-                )
-                dst = coords[i][:, c * N : (c + 1) * N]
-                if i == 0 and c == BANKS - 1:
-                    nc.vector.tensor_copy(out=dst, in_=bank[:])
-                else:
-                    nc.scalar.copy(out=dst, in_=bank[:])
-
-        worth_sb = sb.tile([P, T], F32, align_bytes=64, name="codes0")
-        nc.sync.dma_start(worth_sb[:], worth)
-        old_sb = sb.tile([P, COLS], F32, align_bytes=64, name="codes1")
-        nc.sync.dma_start(old_sb[:], old)
+        last = T - N
+        pieces = [(0, c * N, N, False) for c in range(2)]
+        pieces.extend([(0, 2 * N, N, True), (0, last, N // 2, False), (0, last + N // 2, N // 2, True)])
+        pieces.extend((1, c * N, N, False) for c in range(BANKS))
+        for n, (i, first, cols, on_vector) in enumerate(pieces):
+            bank = psum.tile([P, cols], F32, name=f"bank{n % 8}")
+            half, start = divmod(first, T // 2)
+            nc.tensor.matmul_mx(
+                out=bank[:],
+                lhsT=codes[i][:].bitcast(FP8X4),
+                lhsT_scale=scales[i][:],
+                rhs=keys[half][:, 2 * start : 2 * (start + cols)].bitcast(FP4X4),
+                rhs_scale=key_scales[:, first : first + cols],
+                start=True,
+                stop=True,
+            )
+            dst = coords[i][:, first : first + cols]
+            if on_vector:
+                nc.vector.tensor_copy(out=dst, in_=bank[:])
+            else:
+                nc.scalar.copy(out=dst, in_=bank[:])
 
         def slot_tile(name):
             return sb.tile([P, SLOTS], F32, name=name)
@@ -112,22 +113,20 @@ def tile_attend_planecos_typical_pagesums_kernel(
         }
         halves = [slice(0, SLOTS // 2), slice(SLOTS // 2, SLOTS)]
         list_halves = [slice(0, SLOTS // 32), slice(SLOTS // 32, SLOTS // 16)]
-        for name, tile, window, offsets in (
-            ("a1", a1, coords[0], list1),
-            ("a2", a2, coords[0], list2),
-            ("b1", b1, coords[1], list1),
-        ):
-            nc.vector.tensor_copy(tile[:], window[:].indirect(offsets[:]))
+        for name, tile, offsets in (("a1", a1, list1), ("a2", a2, list2)):
+            nc.vector.tensor_copy(tile[:], coords[0][:].indirect(offsets[:]))
             nc.scalar.activation(sq[name][:], tile[:], ACT.Square)
-        for h, entries in zip(halves, list_halves):
-            nc.vector.tensor_copy(b2[:, h], coords[1][:].indirect(list2[:, entries]))
-            nc.scalar.activation(sq["b2"][:, h], b2[:, h], ACT.Square)
+        for name, tile, offsets in (("b1", b1, list1), ("b2", b2, list2)):
+            for h, entries in zip(halves, list_halves):
+                nc.vector.tensor_copy(tile[:, h], coords[1][:].indirect(offsets[:, entries]))
+                nc.scalar.activation(sq[name][:, h], tile[:, h], ACT.Square)
 
         aa, dot, len1, len2, lens, inv_len, score = (
             slot_tile(n) for n in ("aa", "dot", "len1", "len2", "lens", "inv_len", "score")
         )
-        nc.vector.tensor_tensor(aa[:], a1[:], a2[:], ALU.mult)
-        nc.vector.tensor_tensor(len1[:], sq["a1"][:], sq["b1"][:], ALU.add)
+        nc.gpsimd.tensor_tensor(aa[:], a1[:], a2[:], ALU.mult)
+        for h, engine in zip(halves, (nc.gpsimd, nc.vector)):
+            engine.tensor_tensor(len1[:, h], sq["a1"][:, h], sq["b1"][:, h], ALU.add)
         for h in halves:
             nc.vector.tensor_tensor(len2[:, h], sq["a2"][:, h], sq["b2"][:, h], ALU.add)
             nc.vector.tensor_tensor(b2[:, h], b1[:, h], b2[:, h], ALU.mult)

from contextlib import ExitStack

import concourse.mybir as mybir

F32 = mybir.dt.float32
BF16 = mybir.dt.bfloat16
U32 = mybir.dt.uint32
I32 = mybir.dt.int32
U16 = mybir.dt.uint16
U8 = mybir.dt.uint8
FP8X4 = mybir.dt.float8_e4m3fn_x4
FP4X4 = mybir.dt.float4_e2m1fn_x4
ACT = mybir.ActivationFunctionType
ALU = mybir.AluOpType
AX = mybir.AxisListType

P = 128
PACK = 4
D, T, SLOTS, Q, RUNS, COLS = 512, 2048, 512, 128, 64, 512
RUN = SLOTS // RUNS
N = 512
BANKS = T // N
FLOPS = 2 * 2 * D * Q * T


def tile_attend_planecos_typical_pagesums_kernel(
    tc, query, query2, keys_words, keys_scales, lam, width, worth, old, offs, offs2, offs3, out
):
    nc = tc.nc
    with ExitStack() as ctx:
        sb = ctx.enter_context(tc.tile_pool(name="sb", bufs=1))
        psum = ctx.enter_context(tc.psum_pool(name="psum", bufs=1))

        key_scales = sb.tile([P, T], U8, align_bytes=64)
        warm = sb.tile([P, 1], F32)
        warm_out = sb.tile([P, 1], F32)
        nc.vector.memset(warm[:], 1.0)

        raw = [sb.tile([P, PACK, Q], F32, name=f"raw{i}") for i in range(2)]
        keys = [sb.tile([P, T], U8, align_bytes=64, name=f"keys{h}") for h in range(2)]
        nc.sync.dma_start(out=raw[0][:], in_=query.rearrange("(p j) w -> p j w", j=PACK))
        for quad in range(4):
            nc.sync.dma_start(
                out=key_scales[32 * quad : 32 * quad + 4, :].bitcast(I32),
                in_=keys_scales[0, 4 * quad : 4 * quad + 4, :].bitcast(I32),
            )
        nc.scalar.activation(warm_out[:], warm[:], ACT.Abs_reciprocal_sqrt)
        key_words = keys_words[0].bitcast(I32)
        nc.sync.dma_start(out=keys[0][:].bitcast(I32), in_=key_words[:, : T // 4])
        nc.sync.dma_start(out=raw[1][:], in_=query2.rearrange("(p j) w -> p j w", j=PACK))
        nc.sync.dma_start(out=keys[1][:].bitcast(I32), in_=key_words[:, T // 4 :])

        list1 = sb.tile([P, SLOTS // 16], U16)
        list2 = sb.tile([P, SLOTS // 16], U16)
        list3 = sb.tile([P, RUNS // 16], U16)
        nc.sync.dma_start(list1[:], offs)
        nc.sync.dma_start(list2[:], offs2)
        lam_sb = sb.tile([P, 1], F32)
        width_sb = sb.tile([P, 1], F32)
        worth_sb = sb.tile([P, T], F32)
        old_sb = sb.tile([P, COLS], F32)
        for tile, source in ((list3, offs3), (width_sb, width), (lam_sb, lam), (worth_sb, worth), (old_sb, old)):
            nc.sync.dma_start(tile[:], source)

        placed = sb.tile([P, COLS], F32)
        nc.vector.memset(placed[:], 0.0)

        codes, scales = [], []
        for i in range(2):
            grouped = sb.tile([P, Q, PACK], BF16, align_bytes=64, name=f"grouped{i}")
            nc.vector.tensor_copy(out=grouped[:], in_=raw[i][:].rearrange("p j w -> p w j"))
            codes.append(sb.tile([P, Q], U32, align_bytes=64, name=f"codes{i}"))
            scales.append(sb.tile([P, Q], U8, align_bytes=64, name=f"scales{i}"))
            nc.vector.quantize_mx(
                out=codes[i][:].bitcast(FP8X4), scales=scales[i][:], in_=grouped[:].rearrange("p w j -> p (w j)")
            )

        width2 = sb.tile([P, 1], F32)
        nc.gpsimd.tensor_tensor(width2[:], width_sb[:], width_sb[:], ALU.mult)

        coords = [sb.tile([P, T], F32, name=f"coord{i}") for i in range(2)]
        last = T - N
        pieces = [(0, c * N, N, False) for c in range(2)]
        pieces.extend([(0, 2 * N, N, True), (0, last, N // 2, False), (0, last + N // 2, N // 2, True)])
        pieces.extend((1, c * N, N, False) for c in range(BANKS))
        for n, (i, first, cols, on_vector) in enumerate(pieces):
            bank = psum.tile([P, cols], F32, name=f"bank{n % 8}")
            half, start = divmod(first, T // 2)
            nc.tensor.matmul_mx(
                out=bank[:],
                lhsT=codes[i][:].bitcast(FP8X4),
                lhsT_scale=scales[i][:],
                rhs=keys[half][:, 2 * start : 2 * (start + cols)].bitcast(FP4X4),
                rhs_scale=key_scales[:, first : first + cols],
                start=True,
                stop=True,
            )
            dst = coords[i][:, first : first + cols]
            if on_vector:
                nc.vector.tensor_copy(out=dst, in_=bank[:])
            else:
                nc.scalar.copy(out=dst, in_=bank[:])

        def slot_tile(name):
            return sb.tile([P, SLOTS], F32, name=name)

        a1, a2, b1, b2 = (slot_tile(n) for n in ("a1", "a2", "b1", "b2"))
        sq = {
            "a1": sb.tile([P, SLOTS], F32, align_bytes=64, name="keys1"),
            "a2": sb.tile([P, SLOTS], F32, align_bytes=64, name="key_scales"),
            "b1": slot_tile("sq_b1"),
            "b2": slot_tile("sq_b2"),
        }
        halves = [slice(0, SLOTS // 2), slice(SLOTS // 2, SLOTS)]
        list_halves = [slice(0, SLOTS // 32), slice(SLOTS // 32, SLOTS // 16)]
        for name, tile, offsets in (("a1", a1, list1), ("a2", a2, list2)):
            nc.vector.tensor_copy(tile[:], coords[0][:].indirect(offsets[:]))
            nc.scalar.activation(sq[name][:], tile[:], ACT.Square)
        for name, tile, offsets in (("b1", b1, list1), ("b2", b2, list2)):
            for h, entries in zip(halves, list_halves):
                nc.vector.tensor_copy(tile[:, h], coords[1][:].indirect(offsets[:, entries]))
                nc.scalar.activation(sq[name][:, h], tile[:, h], ACT.Square)

        aa, dot, len1, len2, lens, inv_len, score = (
            slot_tile(n) for n in ("aa", "dot", "len1", "len2", "lens", "inv_len", "score")
        )
        nc.gpsimd.tensor_tensor(aa[:], a1[:], a2[:], ALU.mult)
        for h, engine in zip(halves, (nc.gpsimd, nc.vector)):
            engine.tensor_tensor(len1[:, h], sq["a1"][:, h], sq["b1"][:, h], ALU.add)
        for h in halves:
            nc.vector.tensor_tensor(len2[:, h], sq["a2"][:, h], sq["b2"][:, h], ALU.add)
            nc.vector.tensor_tensor(b2[:, h], b1[:, h], b2[:, h], ALU.mult)
            nc.vector.tensor_tensor(lens[:, h], len1[:, h], len2[:, h], ALU.mult)
            nc.scalar.activation(inv_len[:, h], lens[:, h], ACT.Abs_reciprocal_sqrt, bias=0.5)
        nc.vector.tensor_tensor(dot[:], aa[:], b2[:], ALU.add)
        score_sum = sb.tile([P, 1], F32)
        nc.vector.scalar_tensor_tensor(
            score[:], dot[:], lam_sb[:], inv_len[:], ALU.mult, ALU.mult, accum_out=score_sum[:]
        )

        slot_worth = slot_tile("inv_len")
        nc.vector.tensor_copy(slot_worth[:], worth_sb[:].indirect(list1[:]))

        dev2, root, part, weighed = (slot_tile(n) for n in ("dev2", "root", "part", "weighed"))
        part_sums = [sb.tile([P, 1], F32, name=f"part_sum{i}") for i in range(2)]
        run_sums = sb.tile([P, RUNS], F32)
        for h in halves:
            nc.scalar.activation(dev2[:, h], score[:, h], ACT.Square, bias=score_sum[:], scale=-float(SLOTS))
        for h in halves:
            nc.scalar.activation(root[:, h], dev2[:, h], ACT.Abs_reciprocal_sqrt, bias=width2[:], scale=1.0 / (SLOTS * SLOTS))
        for i, h in enumerate(halves):
            nc.scalar.activation(part[:, h], root[:, h], ACT.Square, accum_out=part_sums[i][:])
        for h in halves:
            nc.vector.tensor_tensor(weighed[:, h], part[:, h], slot_worth[:, h], ALU.mult)
        for i, h in enumerate(halves):
            nc.vector.tensor_reduce(
                run_sums[:, i * RUNS // 2 : (i + 1) * RUNS // 2],
                weighed[:, h].rearrange("p (g r) -> p g r", r=RUN),
                AX.X,
                ALU.add,
            )
        mean_part = sb.tile([P, 1], F32)
        nc.vector.tensor_scalar(mean_part[:], part_sums[0][:], part_sums[1][:], 1.0 / SLOTS, ALU.add, ALU.mult)
        norm = sb.tile([P, 1], F32)
        nc.vector.reciprocal(norm[:], mean_part[:])
        nc.vector.tensor_copy(placed[:].indirect(list3[:]), run_sums[:])
        result = sb.tile([P, COLS], F32)
        for h, queue in zip(halves, (nc.sync, nc.scalar)):
            nc.vector.scalar_tensor_tensor(result[:, h], placed[:, h], norm[:], old_sb[:, h], ALU.mult, ALU.add)
            queue.dma_start(out[:, h], result[:, h])
